import numpy as np
import ml_dtypes

BF16 = ml_dtypes.bfloat16


def bf(x):
    return np.asarray(x, np.float32).astype(BF16)


def f32(x):
    return np.asarray(x, np.float32)


def f64(x):
    return np.asarray(x).astype(np.float64)


def striped(idx):
    return np.concatenate([l.reshape(-1, 16).T for l in idx])


def rows(idx, k):
    return np.tile(np.repeat(idx, 16, axis=0), (k // (16 * 8), 1))


def look(tab, idx):
    return np.take_along_axis(f64(tab), rows(idx, len(tab)), axis=1)


K, S, V, N, M = 128, 2048, 2048, 2048, 128


def setup_inputs():
    return {"tab": f32(np.random.standard_normal((2, K, S))), "y": f32(np.random.standard_normal((K, V))), "w": bf(np.random.standard_normal((K, M)) / np.sqrt(K)), "b": f32(0.5 * np.random.standard_normal((M, 1))), "offs": striped(np.stack([np.random.permutation(S)[:N] for _ in range(8)]))}


def reference(tab, y, w, b, offs):
    idx = np.stack([g.T.reshape(-1) for g in np.split(offs, 8)])
    x = (np.minimum(look(tab[0], idx), f64(y))) * (np.maximum(look(tab[1], idx), 0.0))
    return np.maximum(f64(w).T @ x + f64(b), 0.0)

@@ -1,0 +1,52 @@
+import concourse.mybir as mybir
+
+F32, BF16, U16 = mybir.dt.float32, mybir.dt.bfloat16, mybir.dt.uint16
+MIN, MULT = mybir.AluOpType.min, mybir.AluOpType.mult
+RELU = mybir.ActivationFunctionType.Relu
+
+P = 128
+S = 2048
+N = 2048
+M = 128
+PIECE = 512
+LIST_ROWS = 16
+
+FLOPS = 2 * P * M * N
+
+
+def tile_lookup_vg_minrelu_relu_kernel(tc, tab, y, w, b, offs, out):
+    nc = tc.nc
+    with (
+        tc.tile_pool(name="held", bufs=1) as held,
+        tc.tile_pool(name="ring", bufs=2) as ring,
+        tc.psum_pool(name="psum", bufs=2) as psum,
+    ):
+        offsets = held.tile([P, N // LIST_ROWS], U16)
+        values = held.tile([P, S], F32)
+        gates = held.tile([P, S], F32)
+        stream = held.tile([P, N], F32)
+        weights = held.tile([P, M], BF16)
+        bias = held.tile([M, 1], F32)
+        nc.sync.dma_start(offsets[:], offs)
+        nc.sync.dma_start(values[:], tab[0, :, :])
+        nc.sync.dma_start(gates[:], tab[1, :, :])
+        nc.sync.dma_start(stream[:], y)
+        nc.scalar.dma_start(weights[:], w)
+        nc.scalar.dma_start(bias[:], b)
+
+        for start in range(0, N, PIECE):
+            cols = slice(start, start + PIECE)
+            places = offsets[:, start // LIST_ROWS : (start + PIECE) // LIST_ROWS]
+
+            smaller = ring.tile([P, PIECE], F32)
+            nc.vector.tensor_tensor(smaller[:], values[:].indirect(places), stream[:, cols], MIN)
+            gate = ring.tile([P, PIECE], F32)
+            nc.scalar.activation(gate[:], gates[:].indirect(places), RELU)
+            x = ring.tile([P, PIECE], BF16)
+            nc.vector.tensor_tensor(x[:], smaller[:], gate[:], MULT)
+
+            sums = psum.tile([M, PIECE], F32)
+            nc.tensor.matmul(sums[:], weights[:], x[:], start=True, stop=True)
+            result = ring.tile([M, PIECE], F32)
+            nc.scalar.activation(result[:], sums[:], RELU, bias=bias[:])
+            nc.sync.dma_start(out[:, cols], result[:])

@@ -1,6 +1,7 @@
 import concourse.mybir as mybir
 
 F32, BF16, U16 = mybir.dt.float32, mybir.dt.bfloat16, mybir.dt.uint16
+ADD, MAX = mybir.AluOpType.add, mybir.AluOpType.max
 MIN, MULT = mybir.AluOpType.min, mybir.AluOpType.mult
 RELU = mybir.ActivationFunctionType.Relu
 
@@ -18,35 +19,50 @@ def tile_lookup_vg_minrelu_relu_kernel(tc, tab, y, w, b, offs, out):
     nc = tc.nc
     with (
         tc.tile_pool(name="held", bufs=1) as held,
-        tc.tile_pool(name="ring", bufs=2) as ring,
-        tc.psum_pool(name="psum", bufs=2) as psum,
+        tc.tile_pool(name="ring", bufs=5) as ring,
+        tc.psum_pool(name="psum", bufs=5) as psum,
     ):
         offsets = held.tile([P, N // LIST_ROWS], U16)
         values = held.tile([P, S], F32)
         gates = held.tile([P, S], F32)
-        stream = held.tile([P, N], F32)
+        stream = [held.tile([P, PIECE], F32, name=f"stream{piece}") for piece in range(N // PIECE)]
         weights = held.tile([P, M], BF16)
         bias = held.tile([M, 1], F32)
         nc.sync.dma_start(offsets[:], offs)
         nc.sync.dma_start(values[:], tab[0, :, :])
+        for piece in range(2):
+            nc.sync.dma_start(stream[piece][:], y[:, piece * PIECE : (piece + 1) * PIECE])
         nc.sync.dma_start(gates[:], tab[1, :, :])
-        nc.sync.dma_start(stream[:], y)
+        for piece in range(2, N // PIECE):
+            nc.sync.dma_start(stream[piece][:], y[:, piece * PIECE : (piece + 1) * PIECE])
         nc.scalar.dma_start(weights[:], w)
         nc.scalar.dma_start(bias[:], b)
 
-        for start in range(0, N, PIECE):
+        zero = held.tile([P, 1], F32)
+        nc.vector.memset(zero[:], 0.0)
+        warm = held.tile([P, 1], F32)
+        nc.scalar.activation(warm[:], zero[:], RELU)
+
+        smaller = held.tile([P, N], F32)
+        gate = held.tile([P, N], F32)
+        for piece in range(N // PIECE):
+            start = piece * PIECE
             cols = slice(start, start + PIECE)
             places = offsets[:, start // LIST_ROWS : (start + PIECE) // LIST_ROWS]
+            nc.vector.tensor_tensor(smaller[:, cols], values[:].indirect(places), stream[piece][:], MIN)
+            nc.scalar.activation(gate[:, cols], gates[:].indirect(places), RELU)
 
-            smaller = ring.tile([P, PIECE], F32)
-            nc.vector.tensor_tensor(smaller[:], values[:].indirect(places), stream[:, cols], MIN)
-            gate = ring.tile([P, PIECE], F32)
-            nc.scalar.activation(gate[:], gates[:].indirect(places), RELU)
-            x = ring.tile([P, PIECE], BF16)
-            nc.vector.tensor_tensor(x[:], smaller[:], gate[:], MULT)
-
-            sums = psum.tile([M, PIECE], F32)
+        strips = [slice(start, start + PIECE) for start in range(0, N - PIECE, PIECE)]
+        strips += [slice(N - PIECE, N - PIECE // 2), slice(N - PIECE // 2, N)]
+        for strip, cols in enumerate(strips):
+            width = cols.stop - cols.start
+            x = ring.tile([P, width], BF16)
+            nc.vector.tensor_tensor(x[:], smaller[:, cols], gate[:, cols], MULT)
+            sums = psum.tile([M, width], F32)
             nc.tensor.matmul(sums[:], weights[:], x[:], start=True, stop=True)
-            result = ring.tile([M, PIECE], F32)
-            nc.scalar.activation(result[:], sums[:], RELU, bias=bias[:])
+            result = ring.tile([M, width], F32)
+            if strip % 2 == 0:
+                nc.scalar.activation(result[:], sums[:], RELU, bias=bias[:])
+            else:
+                nc.vector.tensor_scalar(result[:], sums[:], bias[:], 0.0, ADD, MAX)
             nc.sync.dma_start(out[:, cols], result[:])

@@ -20,7 +20,7 @@ def tile_lookup_vg_minrelu_relu_kernel(tc, tab, y, w, b, offs, out):
     with (
         tc.tile_pool(name="held", bufs=1) as held,
         tc.tile_pool(name="ring", bufs=5) as ring,
-        tc.psum_pool(name="psum", bufs=5) as psum,
+        tc.psum_pool(name="psum", bufs=1) as psum,
     ):
         offsets = held.tile([P, N // LIST_ROWS], U16)
         values = held.tile([P, S], F32)
@@ -35,8 +35,8 @@ def tile_lookup_vg_minrelu_relu_kernel(tc, tab, y, w, b, offs, out):
         nc.sync.dma_start(gates[:], tab[1, :, :])
         for piece in range(2, N // PIECE):
             nc.sync.dma_start(stream[piece][:], y[:, piece * PIECE : (piece + 1) * PIECE])
-        nc.scalar.dma_start(weights[:], w)
-        nc.scalar.dma_start(bias[:], b)
+        nc.sync.dma_start(weights[:], w)
+        nc.sync.dma_start(bias[:], b)
 
         zero = held.tile([P, 1], F32)
         nc.vector.memset(zero[:], 0.0)
@@ -54,15 +54,18 @@ def tile_lookup_vg_minrelu_relu_kernel(tc, tab, y, w, b, offs, out):
 
         strips = [slice(start, start + PIECE) for start in range(0, N - PIECE, PIECE)]
         strips += [slice(N - PIECE, N - PIECE // 2), slice(N - PIECE // 2, N)]
+        sums = [psum.tile([M, PIECE], F32, name=f"sums{strip}") for strip in range(len(strips))]
         for strip, cols in enumerate(strips):
             width = cols.stop - cols.start
             x = ring.tile([P, width], BF16)
             nc.vector.tensor_tensor(x[:], smaller[:, cols], gate[:, cols], MULT)
-            sums = psum.tile([M, width], F32)
-            nc.tensor.matmul(sums[:], weights[:], x[:], start=True, stop=True)
+            nc.tensor.matmul(sums[strip][:, :width], weights[:], x[:], start=True, stop=True)
+
+        for strip, cols in enumerate(strips):
+            width = cols.stop - cols.start
             result = ring.tile([M, width], F32)
-            if strip % 2 == 0:
-                nc.scalar.activation(result[:], sums[:], RELU, bias=bias[:])
+            if strip == 0 or strip % 2 == 1:
+                nc.scalar.activation(result[:], sums[strip][:, :width], RELU, bias=bias[:])
             else:
-                nc.vector.tensor_scalar(result[:], sums[:], bias[:], 0.0, ADD, MAX)
+                nc.vector.tensor_scalar(result[:], sums[strip][:, :width], bias[:], 0.0, ADD, MAX)
             nc.sync.dma_start(out[:, cols], result[:])

import concourse.mybir as mybir

F32, BF16, U16 = mybir.dt.float32, mybir.dt.bfloat16, mybir.dt.uint16
ADD, MAX = mybir.AluOpType.add, mybir.AluOpType.max
MIN, MULT = mybir.AluOpType.min, mybir.AluOpType.mult
RELU = mybir.ActivationFunctionType.Relu

P = 128
S = 2048
N = 2048
M = 128
PIECE = 512
LIST_ROWS = 16

FLOPS = 2 * P * M * N


def tile_lookup_vg_minrelu_relu_kernel(tc, tab, y, w, b, offs, out):
    nc = tc.nc
    with (
        tc.tile_pool(name="held", bufs=1) as held,
        tc.tile_pool(name="ring", bufs=5) as ring,
        tc.psum_pool(name="psum", bufs=1) as psum,
    ):
        offsets = held.tile([P, N // LIST_ROWS], U16)
        values = held.tile([P, S], F32)
        gates = held.tile([P, S], F32)
        stream = [held.tile([P, PIECE], F32, name=f"stream{piece}") for piece in range(N // PIECE)]
        weights = held.tile([P, M], BF16)
        bias = held.tile([M, 1], F32)
        nc.sync.dma_start(offsets[:], offs)
        nc.sync.dma_start(values[:], tab[0, :, :])
        for piece in range(2):
            nc.sync.dma_start(stream[piece][:], y[:, piece * PIECE : (piece + 1) * PIECE])
        nc.sync.dma_start(gates[:], tab[1, :, :])
        for piece in range(2, N // PIECE):
            nc.sync.dma_start(stream[piece][:], y[:, piece * PIECE : (piece + 1) * PIECE])
        nc.sync.dma_start(weights[:], w)
        nc.sync.dma_start(bias[:], b)

        zero = held.tile([P, 1], F32)
        nc.vector.memset(zero[:], 0.0)
        warm = held.tile([P, 1], F32)
        nc.scalar.activation(warm[:], zero[:], RELU)

        smaller = held.tile([P, N], F32)
        gate = held.tile([P, N], F32)
        for piece in range(N // PIECE):
            start = piece * PIECE
            cols = slice(start, start + PIECE)
            places = offsets[:, start // LIST_ROWS : (start + PIECE) // LIST_ROWS]
            nc.vector.tensor_tensor(smaller[:, cols], values[:].indirect(places), stream[piece][:], MIN)
            nc.scalar.activation(gate[:, cols], gates[:].indirect(places), RELU)

        strips = [slice(start, start + PIECE) for start in range(0, N - PIECE, PIECE)]
        strips += [slice(N - PIECE, N - PIECE // 2), slice(N - PIECE // 2, N)]
        sums = [psum.tile([M, PIECE], F32, name=f"sums{strip}") for strip in range(len(strips))]
        for strip, cols in enumerate(strips):
            width = cols.stop - cols.start
            x = ring.tile([P, width], BF16)
            nc.vector.tensor_tensor(x[:], smaller[:, cols], gate[:, cols], MULT)
            nc.tensor.matmul(sums[strip][:, :width], weights[:], x[:], start=True, stop=True)

        for strip, cols in enumerate(strips):
            width = cols.stop - cols.start
            result = ring.tile([M, width], F32)
            if strip == 0 or strip % 2 == 1:
                nc.scalar.activation(result[:], sums[strip][:, :width], RELU, bias=bias[:])
            else:
                nc.vector.tensor_scalar(result[:], sums[strip][:, :width], bias[:], 0.0, ADD, MAX)
            nc.sync.dma_start(out[:, cols], result[:])
